import numpy as np
import ml_dtypes


def mxq(x, axis, fmt="e4m3"):
    dtype, down = {"e4m3": (ml_dtypes.float8_e4m3fn, 7), "e5m2": (ml_dtypes.float8_e5m2, 14)}[fmt]
    v = np.moveaxis(np.asarray(x, np.float32).astype(ml_dtypes.bfloat16).astype(np.float64), axis, -1)
    blocks = v.reshape(v.shape[:-1] + (-1, 32))
    amax = np.abs(blocks).max(-1, keepdims=True)
    byte = np.maximum(np.where(amax > 0, np.frexp(amax)[1] - 1 + 127, 0) - down, 1)
    scale = np.exp2(byte - 127.0)
    codes = (blocks / scale).astype(np.float32).astype(dtype).astype(np.float64)
    return np.moveaxis((codes * scale).reshape(v.shape), -1, axis)


WIDE = False


def mx_kscale(k):
    if not WIDE:
        return np.ones(k)
    levels = np.array([30, -30])
    if k % 512:
        return np.exp2(np.random.permutation(np.resize(levels, k // 32))).repeat(32)
    a = np.empty((k // 512, 16))
    for p in range(k // 512):
        a[p, :8] = np.random.permutation(np.resize(levels, 8))
        for g in range(8):
            far = levels[np.abs(levels - a[p, g]) >= 10]
            a[p, g + 8] = far[np.random.randint(len(far))]
    return np.exp2(a.ravel()).repeat(32)


def f64(x):
    return np.asarray(x).astype(np.float64)


E2M1 = np.array([0.0, 0.5, 1.0, 1.5, 2.0, 3.0, 4.0, 6.0, -0.0, -0.5, -1.0, -1.5, -2.0, -3.0, -4.0, -6.0])


def pack_weight(w, fmt):
    k, n = w.shape
    w = f64(np.asarray(w, np.float32).astype(ml_dtypes.bfloat16)).reshape(k // 32, 32, n)
    amax = np.abs(w).max(1)
    if fmt == "e4m3":
        byte = np.frexp(amax)[1] - 1 + 127 - 7
    else:
        mant, ex = np.frexp(amax / 6.0)
        byte = np.where(mant > 0.5, ex, ex - 1) + 127
    byte = np.clip(np.where(amax > 0, byte, 1), 1, 254)
    scaled = (w * np.exp2(127.0 - byte)[:, None, :]).reshape(k, n).astype(np.float32)
    by_word = np.ascontiguousarray(scaled.reshape(k // 512, 128, 4, n).transpose(0, 1, 3, 2))
    if fmt == "e4m3":
        words = by_word.astype(ml_dtypes.float8_e4m3fn).view(np.uint8)
    else:
        c = by_word.astype(ml_dtypes.float4_e2m1fn).view(np.uint8) & 0xF
        words = (c[..., 0::2] | (c[..., 1::2] << 4)).reshape(k // 512, 128, 2 * n)
    return np.ascontiguousarray(words), np.ascontiguousarray(byte.astype(np.uint8).reshape(k // 512, 16, n))


def unpack_weight(words, scales, fmt):
    g, _, n = scales.shape
    words = np.ascontiguousarray(words).reshape(g, 128, n, -1)
    if fmt == "e4m3":
        vals = words.view(ml_dtypes.float8_e4m3fn).astype(np.float64)
    else:
        nib = np.empty((g, 128, n, 4), np.uint8)
        nib[..., 0::2] = words & 0xF
        nib[..., 1::2] = words >> 4
        vals = E2M1[nib]
    vals = vals * np.repeat(np.exp2(scales.astype(np.float64) - 127.0), 8, axis=1)[..., None]
    return vals.transpose(0, 1, 3, 2).reshape(g * 512, n)


K, R, N, T, S = 512, 512, 1024, 512, 512


def setup_inputs():
    n = np.random.standard_normal
    ft = mx_kscale(T)
    fn = mx_kscale(N)
    fs = mx_kscale(S)
    wdp = pack_weight(n((N, R)) * 1 / np.sqrt(N) * fn[:, None], "e2m1")
    xsp = pack_weight(n((S, K)) * fs[:, None], "e4m3")
    gsp = pack_weight(n((S, R)) / fs[:, None], "e2m1")
    return {
        "xr": (n((T, K)) * ft[:, None]).astype(np.float32),
        "g": (n((N, T)) * np.exp(0.5 * n((1, T))) / fn[:, None]).astype(np.float32),
        "wd_words": wdp[0],
        "wd_scales": wdp[1],
        "sv": (n((R, T))).astype(np.float32),
        "rw": (np.random.uniform(0.4, 1.2, (1, T)) / ft).astype(np.float32),
        "xs_words": xsp[0],
        "xs_scales": xsp[1],
        "gs_words": gsp[0],
        "gs_scales": gsp[1],
    }


def reference(xr, g, wd_words, wd_scales, sv, rw, xs_words, xs_scales, gs_words, gs_scales):
    wdu = unpack_weight(wd_words, wd_scales, "e2m1")
    xsu = unpack_weight(xs_words, xs_scales, "e4m3")
    gsu = unpack_weight(gs_words, gs_scales, "e2m1")
    gq = mxq(f64(g), 0, "e5m2")
    d = wdu.T @ gq
    dz = d * np.maximum(f64(sv), 0.0) * f64(rw)
    dt1 = dz.T
    xrq = mxq(f64(xr), 0, "e4m3")
    dt1q = mxq(dt1, 0, "e5m2")
    w = xrq.T @ dt1q + xsu.T @ gsu
    y = 0.04 * w
    return y

@@ -1,0 +1,286 @@
+from contextlib import ExitStack
+
+import concourse.mybir as mybir
+from concourse.masks import make_identity
+
+K, R, N, T, S = 512, 512, 1024, 512, 512
+FLOPS = 2 * (N * R * T + T * K * R + S * K * R)
+
+F32 = mybir.dt.float32
+BF16 = mybir.dt.bfloat16
+I32 = mybir.dt.int32
+U32 = mybir.dt.uint32
+U8 = mybir.dt.uint8
+E4M3 = mybir.dt.float8_e4m3fn_x4
+E5M2 = mybir.dt.float8_e5m2_x4
+E2M1 = mybir.dt.float4_e2m1fn_x4
+ALU = mybir.AluOpType
+ACT = mybir.ActivationFunctionType
+
+P = 128
+PACK = 4
+HALF = 256
+TILES = 4
+OUT_SCALE = 0.04
+G_CUTS = [[0, 256, 512], [0, 256, 384, 512]]
+OUT_CUTS = [[0, 256, 512], [0, 512], [0, 512], [0, 512]]
+X_CUTS = [0, 256, 512]
+
+
+def tile_mix_first_layer_wgrad_with_store_kernel(
+    tc, xr, g, wd_words, wd_scales, sv, rw, xs_words, xs_scales, gs_words, gs_scales, out
+):
+    nc = tc.nc
+    with ExitStack() as ctx:
+        sb = ctx.enter_context(tc.tile_pool(name="sb", bufs=1))
+        ps = ctx.enter_context(tc.psum_pool(name="ps", bufs=1))
+        ctx.enter_context(tc.manual_schedule())
+
+        def sbuf(name, shape, dtype):
+            return sb.tile(shape, dtype, name=name, align_bytes=64)
+
+        ident = sbuf("ident", [P, P], F32)
+        make_identity(nc, ident[:])
+        wd_plane = sbuf("wd_plane", [P, 2, R], U8)
+        xs_plane = sbuf("xs_plane", [P, K], U8)
+        gs_plane = sbuf("gs_plane", [P, R], U8)
+        nc.vector.memset(wd_plane[:].rearrange("p z c -> p (z c)").bitcast(I32), 0)
+        nc.vector.memset(xs_plane[:].bitcast(I32), 0)
+        nc.vector.memset(gs_plane[:].bitcast(I32), 0)
+
+        rw_col = sbuf("rw_col", [P, PACK], F32)
+        g_raw = [
+            [sbuf("g_raw%d%d" % (z, h), [P, PACK, cuts[h + 1] - cuts[h]], F32) for h in range(len(cuts) - 1)]
+            for z, cuts in enumerate(G_CUTS)
+        ]
+        xr_raw = [sbuf("xr_raw%d" % h, [P, PACK, HALF], F32) for h in range(2)]
+        sv_raw = [sbuf("sv_raw%d" % i, [P, T], F32) for i in range(TILES)]
+        wd_codes = [sbuf("wd_codes%d" % z, [P, 2 * R], U8) for z in range(2)]
+        xs_codes = sbuf("xs_codes", [P, K], U32)
+        gs_codes = sbuf("gs_codes", [P, 2 * R], U8)
+
+        def load_rows(raw, rows, cols):
+            nc.sync.dma_start(out=raw[:], in_=rows.rearrange("(p j) w -> p j w", j=PACK)[:, :, cols])
+
+        def load_g(z, h):
+            load_rows(g_raw[z][h], g[512 * z : 512 * (z + 1), :], slice(G_CUTS[z][h], G_CUTS[z][h + 1]))
+
+        def load_xr(h):
+            load_rows(xr_raw[h], xr, slice(HALF * h, HALF * (h + 1)))
+
+        def load_sv(i):
+            nc.sync.dma_start(out=sv_raw[i][:], in_=sv[i * P : (i + 1) * P, :])
+
+        def load_rw():
+            nc.sync.dma_start(out=rw_col[:], in_=rw[0].rearrange("(p j) -> p j", j=PACK))
+
+        def load_bytes(codes, words):
+            nc.sync.dma_start(out=codes[:].bitcast(I32), in_=words.bitcast(I32))
+
+        def load_plane(plane, scales, queue):
+            for q in range(4):
+                queue.dma_start(
+                    out=plane[32 * q : 32 * q + 4].bitcast(I32),
+                    in_=scales[4 * q : 4 * q + 4].bitcast(I32),
+                )
+
+        load_plane(xs_plane, xs_scales[0], nc.gpsimd)
+        load_rw()
+        load_sv(0)
+        load_sv(1)
+        load_sv(2)
+        load_g(0, 0)
+        load_g(0, 1)
+        load_bytes(wd_codes[0], wd_words[0])
+        load_plane(wd_plane, wd_scales.rearrange("z q c -> q z c"), nc.sync)
+        load_g(1, 0)
+        load_g(1, 1)
+        load_g(1, 2)
+        load_bytes(wd_codes[1], wd_words[1])
+        load_sv(3)
+        load_xr(0)
+        load_plane(gs_plane, gs_scales[0], nc.sync)
+        load_bytes(xs_codes, xs_words[0].rearrange("p c t -> p (c t)"))
+        load_bytes(gs_codes, gs_words[0])
+        load_xr(1)
+
+        rw_all = ps.tile([P, PACK, P], F32, name="rw_all", tag="w3")
+        g_bf = [
+            [sbuf("g_bf%d%d" % (z, h), [P, cuts[h + 1] - cuts[h], PACK], BF16) for h in range(len(cuts) - 1)]
+            for z, cuts in enumerate(G_CUTS)
+        ]
+        g_codes = [sbuf("g_codes%d" % z, [P, T], U32) for z in range(2)]
+        g_plane = [sbuf("g_plane%d" % z, [P, T], U8) for z in range(2)]
+        d_bank = [ps.tile([P, T], F32, name="d%d" % i, tag="d%d" % i) for i in range(TILES)]
+        gate = [sbuf("gate%d" % i, [P, T], F32) for i in range(TILES)]
+        dz = [sbuf("dz%d" % i, [P, T], BF16) for i in range(TILES)]
+        dt_bf = [sbuf("dt_bf%d" % i, [P, P, PACK], BF16) for i in range(TILES)]
+        dt_codes = sbuf("dt_codes", [P, R], U32)
+        dt_plane = sbuf("dt_plane", [P, R], U8)
+        xr_codes = [sbuf("xr_codes%d" % h, [P, HALF], U32) for h in range(2)]
+        xr_plane = [sbuf("xr_plane%d" % h, [P, HALF], U8) for h in range(2)]
+        xr_bf = [sbuf("xr_bf%d" % h, [P, HALF, PACK], BF16) for h in range(2)]
+        turned = {}
+        w_bank = {}
+
+        def spread_rw():
+            for j in range(PACK):
+                nc.tensor.transpose(rw_all[:, j, :], rw_col[:, j : j + 1].to_broadcast([P, P]), ident[:])
+
+        def interleave(copy, grouped, raw, c0, c1):
+            copy(
+                out=grouped[:, c0:c1, :].rearrange("p (c i) j -> p c j i", i=4),
+                in_=raw[:, :, c0:c1].rearrange("p j (c i) -> p c j i", i=4),
+            )
+
+        def cast(grouped, raw, share):
+            if share > 0:
+                interleave(nc.vector.tensor_copy, grouped, raw, 0, share)
+            if share < raw.shape[2]:
+                interleave(nc.scalar.copy, grouped, raw, share, raw.shape[2])
+
+        def quantize(grouped, codes, plane, fmt):
+            nc.vector.quantize_mx(out=codes.bitcast(fmt), scales=plane, in_=grouped[:].rearrange("p c j -> p (c j)"))
+
+        def cast_g(z, h, share):
+            cast(g_bf[z][h], g_raw[z][h], share)
+
+        def quantize_g(z, h):
+            cols = slice(G_CUTS[z][h], G_CUTS[z][h + 1])
+            quantize(g_bf[z][h], g_codes[z][:, cols], g_plane[z][:, cols], E5M2)
+
+        def cast_xr(h, share):
+            cast(xr_bf[h], xr_raw[h], share)
+
+        def quantize_xr(h):
+            quantize(xr_bf[h], xr_codes[h][:], xr_plane[h][:], E4M3)
+
+        def d_pass(i, z):
+            nc.tensor.matmul_mx(
+                out=d_bank[i][:],
+                lhsT=wd_codes[z][:, 2 * P * i : 2 * P * (i + 1)].bitcast(E2M1),
+                lhsT_scale=wd_plane[:, z, P * i : P * (i + 1)],
+                rhs=g_codes[z][:].bitcast(E5M2),
+                rhs_scale=g_plane[z][:],
+                start=(z == 0),
+                stop=(z == 1),
+            )
+
+        def make_gate(i):
+            nc.vector.scalar_tensor_tensor(
+                out=gate[i][:].rearrange("p (n j) -> p n j", j=PACK),
+                in0=sv_raw[i][:].rearrange("p (n j) -> p n j", j=PACK),
+                scalar=0.0,
+                in1=rw_all[:].rearrange("p j n -> p n j"),
+                op0=ALU.max,
+                op1=ALU.mult,
+            )
+
+        def make_dz(i):
+            nc.vector.tensor_tensor(out=dz[i][:], in0=d_bank[i][:], in1=gate[i][:], op=ALU.mult)
+
+        def turn(i):
+            words = dz[i][:].bitcast(F32)
+            turned[i] = ps.tile([P, 2, P], F32, name="turned%d" % i, tag="d%d" % i)
+            for u in range(2):
+                nc.tensor.transpose(turned[i][:, u, :], words[:, u : HALF : 2], ident[:])
+
+        def fetch(i):
+            nc.scalar.copy(out=dt_bf[i][:].bitcast(F32), in_=turned[i][:].rearrange("p u r -> p r u"))
+
+        def quantize_dt(i):
+            cols = slice(i * P, (i + 1) * P)
+            quantize(dt_bf[i], dt_codes[:, cols], dt_plane[:, cols], E5M2)
+
+        def stored_pass(i):
+            cols = slice(i * P, (i + 1) * P)
+            w_bank[i] = ps.tile([P, R], F32, name="w%d" % i, tag="w%d" % i)
+            nc.tensor.matmul_mx(
+                out=w_bank[i][:],
+                lhsT=xs_codes[:, cols].bitcast(E4M3),
+                lhsT_scale=xs_plane[:, cols],
+                rhs=gs_codes[:].bitcast(E2M1),
+                rhs_scale=gs_plane[:],
+                start=True,
+                stop=False,
+            )
+
+        def fresh_pass(i):
+            cols = slice((i % 2) * P, (i % 2 + 1) * P)
+            nc.tensor.matmul_mx(
+                out=w_bank[i][:],
+                lhsT=xr_codes[i // 2][:, cols].bitcast(E4M3),
+                lhsT_scale=xr_plane[i // 2][:, cols],
+                rhs=dt_codes[:].bitcast(E5M2),
+                rhs_scale=dt_plane[:],
+                start=False,
+                stop=True,
+            )
+
+        def store(i):
+            cuts = OUT_CUTS[i]
+            for c0, c1 in zip(cuts, cuts[1:]):
+                result = sbuf("result%d_%d" % (i, c0), [P, c1 - c0], F32)
+                if i % 2 == 0:
+                    nc.scalar.activation(out=result[:], in_=w_bank[i][:, c0:c1], func=ACT.Copy, scale=OUT_SCALE)
+                else:
+                    nc.vector.tensor_scalar(
+                        out=result[:], in0=w_bank[i][:, c0:c1], scalar1=OUT_SCALE, scalar2=None, op0=ALU.mult
+                    )
+                nc.sync.dma_start(out=out[i * P : (i + 1) * P, c0:c1], in_=result[:])
+
+        spread_rw()
+        make_gate(0)
+        make_gate(1)
+        make_gate(2)
+        cast_g(0, 0, 0)
+        cast_g(0, 1, 128)
+        quantize_g(0, 0)
+        quantize_g(0, 1)
+        d_pass(0, 0)
+        d_pass(1, 0)
+        d_pass(2, 0)
+        d_pass(3, 0)
+        cast_g(1, 0, 160)
+        quantize_g(1, 0)
+        cast_g(1, 1, 0)
+        cast_g(1, 2, 128)
+        quantize_g(1, 1)
+        quantize_g(1, 2)
+        d_pass(0, 1)
+        d_pass(1, 1)
+        d_pass(2, 1)
+        d_pass(3, 1)
+        make_gate(3)
+        cast_xr(0, 0)
+        make_dz(0)
+        turn(0)
+        make_dz(1)
+        turn(1)
+        make_dz(2)
+        stored_pass(0)
+        stored_pass(1)
+        turn(2)
+        make_dz(3)
+        turn(3)
+        stored_pass(2)
+        stored_pass(3)
+        fetch(0)
+        fetch(1)
+        fetch(2)
+        fetch(3)
+        quantize_xr(0)
+        quantize_dt(0)
+        quantize_dt(1)
+        cast_xr(1, 256)
+        quantize_dt(2)
+        quantize_xr(1)
+        quantize_dt(3)
+        fresh_pass(0)
+        store(0)
+        fresh_pass(1)
+        store(1)
+        fresh_pass(2)
+        store(2)
+        fresh_pass(3)
+        store(3)

@@ -22,7 +22,7 @@ PACK = 4
 HALF = 256
 TILES = 4
 OUT_SCALE = 0.04
-G_CUTS = [[0, 256, 512], [0, 256, 384, 512]]
+G_CUTS = [[0, 256, 512], [0, 256, 512]]
 OUT_CUTS = [[0, 256, 512], [0, 512], [0, 512], [0, 512]]
 X_CUTS = [0, 256, 512]
 
@@ -49,12 +49,12 @@ def tile_mix_first_layer_wgrad_with_store_kernel(
         nc.vector.memset(gs_plane[:].bitcast(I32), 0)
 
         rw_col = sbuf("rw_col", [P, PACK], F32)
-        g_raw = [
-            [sbuf("g_raw%d%d" % (z, h), [P, PACK, cuts[h + 1] - cuts[h]], F32) for h in range(len(cuts) - 1)]
-            for z, cuts in enumerate(G_CUTS)
-        ]
+        g_first = sbuf("g_first", [P, PACK, T], F32)
+        g_second = [sbuf("g_second%d" % h, [P, PACK, HALF], F32) for h in range(2)]
+        g_raw = [[g_first[:, :, 0:HALF], g_first[:, :, HALF:T]], g_second]
         xr_raw = [sbuf("xr_raw%d" % h, [P, PACK, HALF], F32) for h in range(2)]
-        sv_raw = [sbuf("sv_raw%d" % i, [P, T], F32) for i in range(TILES)]
+        sv_early = sbuf("sv_early", [P, 3, T], F32)
+        sv_raw = [sv_early[:, i, :] for i in range(3)] + [sbuf("sv_raw%d" % i, [P, T], F32) for i in range(3, TILES)]
         wd_codes = [sbuf("wd_codes%d" % z, [P, 2 * R], U8) for z in range(2)]
         xs_codes = sbuf("xs_codes", [P, K], U32)
         gs_codes = sbuf("gs_codes", [P, 2 * R], U8)
@@ -72,7 +72,7 @@ def tile_mix_first_layer_wgrad_with_store_kernel(
             nc.sync.dma_start(out=sv_raw[i][:], in_=sv[i * P : (i + 1) * P, :])
 
         def load_rw():
-            nc.sync.dma_start(out=rw_col[:], in_=rw[0].rearrange("(p j) -> p j", j=PACK))
+            nc.scalar.dma_start(out=rw_col[:], in_=rw[0].rearrange("(p j) -> p j", j=PACK))
 
         def load_bytes(codes, words):
             nc.sync.dma_start(out=codes[:].bitcast(I32), in_=words.bitcast(I32))
@@ -86,16 +86,12 @@ def tile_mix_first_layer_wgrad_with_store_kernel(
 
         load_plane(xs_plane, xs_scales[0], nc.gpsimd)
         load_rw()
-        load_sv(0)
-        load_sv(1)
-        load_sv(2)
-        load_g(0, 0)
-        load_g(0, 1)
+        nc.sync.dma_start(out=sv_early[:], in_=sv[0 : 3 * P, :].rearrange("(i p) t -> p i t", p=P))
+        load_rows(g_first, g[0:512, :], slice(0, T))
         load_bytes(wd_codes[0], wd_words[0])
-        load_plane(wd_plane, wd_scales.rearrange("z q c -> q z c"), nc.sync)
+        load_plane(wd_plane, wd_scales.rearrange("z q c -> q z c"), nc.scalar)
         load_g(1, 0)
         load_g(1, 1)
-        load_g(1, 2)
         load_bytes(wd_codes[1], wd_words[1])
         load_sv(3)
         load_xr(0)
@@ -233,8 +229,8 @@ def tile_mix_first_layer_wgrad_with_store_kernel(
         make_gate(0)
         make_gate(1)
         make_gate(2)
-        cast_g(0, 0, 0)
-        cast_g(0, 1, 128)
+        cast_g(0, 0, 160)
+        cast_g(0, 1, 160)
         quantize_g(0, 0)
         quantize_g(0, 1)
         d_pass(0, 0)
@@ -243,10 +239,8 @@ def tile_mix_first_layer_wgrad_with_store_kernel(
         d_pass(3, 0)
         cast_g(1, 0, 160)
         quantize_g(1, 0)
-        cast_g(1, 1, 0)
-        cast_g(1, 2, 128)
+        cast_g(1, 1, 160)
         quantize_g(1, 1)
-        quantize_g(1, 2)
         d_pass(0, 1)
         d_pass(1, 1)
         d_pass(2, 1)

@@ -49,12 +49,13 @@ def tile_mix_first_layer_wgrad_with_store_kernel(
         nc.vector.memset(gs_plane[:].bitcast(I32), 0)
 
         rw_col = sbuf("rw_col", [P, PACK], F32)
-        g_first = sbuf("g_first", [P, PACK, T], F32)
-        g_second = [sbuf("g_second%d" % h, [P, PACK, HALF], F32) for h in range(2)]
-        g_raw = [[g_first[:, :, 0:HALF], g_first[:, :, HALF:T]], g_second]
+        g_raw = [
+            [sbuf("g_raw%d%d" % (z, h), [P, PACK, cuts[h + 1] - cuts[h]], F32) for h in range(len(cuts) - 1)]
+            for z, cuts in enumerate(G_CUTS)
+        ]
         xr_raw = [sbuf("xr_raw%d" % h, [P, PACK, HALF], F32) for h in range(2)]
-        sv_early = sbuf("sv_early", [P, 3, T], F32)
-        sv_raw = [sv_early[:, i, :] for i in range(3)] + [sbuf("sv_raw%d" % i, [P, T], F32) for i in range(3, TILES)]
+        sv_early = sbuf("sv_early", [P, 2, T], F32)
+        sv_raw = [sv_early[:, i, :] for i in range(2)] + [sbuf("sv_raw%d" % i, [P, T], F32) for i in range(2, TILES)]
         wd_codes = [sbuf("wd_codes%d" % z, [P, 2 * R], U8) for z in range(2)]
         xs_codes = sbuf("xs_codes", [P, K], U32)
         gs_codes = sbuf("gs_codes", [P, 2 * R], U8)
@@ -85,17 +86,19 @@ def tile_mix_first_layer_wgrad_with_store_kernel(
                 )
 
         load_plane(xs_plane, xs_scales[0], nc.gpsimd)
+        load_plane(gs_plane, gs_scales[0], nc.gpsimd)
         load_rw()
-        nc.sync.dma_start(out=sv_early[:], in_=sv[0 : 3 * P, :].rearrange("(i p) t -> p i t", p=P))
-        load_rows(g_first, g[0:512, :], slice(0, T))
+        nc.sync.dma_start(out=sv_early[:], in_=sv[0 : 2 * P, :].rearrange("(i p) t -> p i t", p=P))
+        load_g(0, 0)
+        load_g(0, 1)
         load_bytes(wd_codes[0], wd_words[0])
         load_plane(wd_plane, wd_scales.rearrange("z q c -> q z c"), nc.scalar)
         load_g(1, 0)
         load_g(1, 1)
         load_bytes(wd_codes[1], wd_words[1])
+        load_sv(2)
         load_sv(3)
         load_xr(0)
-        load_plane(gs_plane, gs_scales[0], nc.sync)
         load_bytes(xs_codes, xs_words[0].rearrange("p c t -> p (c t)"))
         load_bytes(gs_codes, gs_words[0])
         load_xr(1)
@@ -163,23 +166,48 @@ def tile_mix_first_layer_wgrad_with_store_kernel(
             )
 
         def make_gate(i):
-            nc.vector.scalar_tensor_tensor(
-                out=gate[i][:].rearrange("p (n j) -> p n j", j=PACK),
-                in0=sv_raw[i][:].rearrange("p (n j) -> p n j", j=PACK),
-                scalar=0.0,
-                in1=rw_all[:].rearrange("p j n -> p n j"),
-                op0=ALU.max,
-                op1=ALU.mult,
+            for u in range(2):
+                nc.vector.scalar_tensor_tensor(
+                    out=gate[i][:, HALF * u : HALF * (u + 1)].rearrange("p (m e) -> p m e", e=2),
+                    in0=sv_raw[i][:].rearrange("p (m j) -> p m j", j=PACK)[:, :, 2 * u : 2 * u + 2],
+                    scalar=0.0,
+                    in1=rw_all[:, 2 * u : 2 * u + 2, :].rearrange("p e m -> p m e"),
+                    op0=ALU.max,
+                    op1=ALU.mult,
+                )
+
+        rw_row = sbuf("rw_row", [P, T], F32)
+        sv_pos = sbuf("sv_pos", [P, T], F32)
+
+        def fetch_rw():
+            nc.scalar.copy(
+                out=rw_row[:].rearrange("p (u m e) -> p u m e", u=2, e=2),
+                in_=rw_all[:].rearrange("p (u e) m -> p u m e", e=2),
             )
 
+        def relu(i):
+            nc.scalar.activation(
+                out=sv_pos[:].rearrange("p (u m e) -> p u m e", u=2, e=2),
+                in_=sv_raw[i][:].rearrange("p (m u e) -> p u m e", u=2, e=2),
+                func=ACT.Relu,
+            )
+
+        def pool_gate(i):
+            nc.gpsimd.tensor_tensor(out=gate[i][:], in0=sv_pos[:], in1=rw_row[:], op=ALU.mult)
+
         def make_dz(i):
-            nc.vector.tensor_tensor(out=dz[i][:], in0=d_bank[i][:], in1=gate[i][:], op=ALU.mult)
+            nc.vector.tensor_tensor(
+                out=dz[i][:].rearrange("p (u m e) -> p u m e", u=2, e=2),
+                in0=d_bank[i][:].rearrange("p (m u e) -> p u m e", u=2, e=2),
+                in1=gate[i][:].rearrange("p (u m e) -> p u m e", u=2, e=2),
+                op=ALU.mult,
+            )
 
         def turn(i):
             words = dz[i][:].bitcast(F32)
             turned[i] = ps.tile([P, 2, P], F32, name="turned%d" % i, tag="d%d" % i)
             for u in range(2):
-                nc.tensor.transpose(turned[i][:, u, :], words[:, u : HALF : 2], ident[:])
+                nc.tensor.transpose(turned[i][:, u, :], words[:, P * u : P * (u + 1)], ident[:])
 
         def fetch(i):
             nc.scalar.copy(out=dt_bf[i][:].bitcast(F32), in_=turned[i][:].rearrange("p u r -> p r u"))
@@ -228,11 +256,11 @@ def tile_mix_first_layer_wgrad_with_store_kernel(
         spread_rw()
         make_gate(0)
         make_gate(1)
-        make_gate(2)
-        cast_g(0, 0, 160)
-        cast_g(0, 1, 160)
+        cast_g(0, 0, 128)
         quantize_g(0, 0)
+        cast_g(0, 1, 160)
         quantize_g(0, 1)
+        fetch_rw()
         d_pass(0, 0)
         d_pass(1, 0)
         d_pass(2, 0)
@@ -245,20 +273,21 @@ def tile_mix_first_layer_wgrad_with_store_kernel(
         d_pass(1, 1)
         d_pass(2, 1)
         d_pass(3, 1)
-        make_gate(3)
+        relu(3)
+        pool_gate(3)
+        make_gate(2)
         cast_xr(0, 0)
         make_dz(0)
         turn(0)
         make_dz(1)
         turn(1)
         make_dz(2)
-        stored_pass(0)
-        stored_pass(1)
         turn(2)
+        stored_pass(0)
         make_dz(3)
         turn(3)
+        stored_pass(1)
         stored_pass(2)
-        stored_pass(3)
         fetch(0)
         fetch(1)
         fetch(2)
@@ -266,15 +295,16 @@ def tile_mix_first_layer_wgrad_with_store_kernel(
         quantize_xr(0)
         quantize_dt(0)
         quantize_dt(1)
-        cast_xr(1, 256)
         quantize_dt(2)
-        quantize_xr(1)
         quantize_dt(3)
+        cast_xr(1, 160)
+        quantize_xr(1)
         fresh_pass(0)
         store(0)
         fresh_pass(1)
         store(1)
         fresh_pass(2)
         store(2)
+        stored_pass(3)
         fresh_pass(3)
         store(3)

@@ -19,12 +19,14 @@ ACT = mybir.ActivationFunctionType
 
 P = 128
 PACK = 4
+PASS = P * PACK
 HALF = 256
 TILES = 4
+EARLY = 2
+VECTOR_GATE = 2
+GPSIMD_GATE = 3
+CAST_SHARE = 160
 OUT_SCALE = 0.04
-G_CUTS = [[0, 256, 512], [0, 256, 512]]
-OUT_CUTS = [[0, 256, 512], [0, 512], [0, 512], [0, 512]]
-X_CUTS = [0, 256, 512]
 
 
 def tile_mix_first_layer_wgrad_with_store_kernel(
@@ -39,8 +41,15 @@ def tile_mix_first_layer_wgrad_with_store_kernel(
         def sbuf(name, shape, dtype):
             return sb.tile(shape, dtype, name=name, align_bytes=64)
 
+        def tile_cols(i):
+            return slice(P * i, P * (i + 1))
+
+        def half_cols(h):
+            return slice(HALF * h, HALF * (h + 1))
+
         ident = sbuf("ident", [P, P], F32)
         make_identity(nc, ident[:])
+
         wd_plane = sbuf("wd_plane", [P, 2, R], U8)
         xs_plane = sbuf("xs_plane", [P, K], U8)
         gs_plane = sbuf("gs_plane", [P, R], U8)
@@ -49,82 +58,74 @@ def tile_mix_first_layer_wgrad_with_store_kernel(
         nc.vector.memset(gs_plane[:].bitcast(I32), 0)
 
         rw_col = sbuf("rw_col", [P, PACK], F32)
-        g_raw = [
-            [sbuf("g_raw%d%d" % (z, h), [P, PACK, cuts[h + 1] - cuts[h]], F32) for h in range(len(cuts) - 1)]
-            for z, cuts in enumerate(G_CUTS)
-        ]
+        g_raw = [[sbuf("g_raw%d%d" % (z, h), [P, PACK, HALF], F32) for h in range(2)] for z in range(2)]
         xr_raw = [sbuf("xr_raw%d" % h, [P, PACK, HALF], F32) for h in range(2)]
-        sv_early = sbuf("sv_early", [P, 2, T], F32)
-        sv_raw = [sv_early[:, i, :] for i in range(2)] + [sbuf("sv_raw%d" % i, [P, T], F32) for i in range(2, TILES)]
+        sv_early = sbuf("sv_early", [P, EARLY, T], F32)
+        sv_late = [sbuf("sv_late%d" % i, [P, T], F32) for i in range(EARLY, TILES)]
+        sv_raw = [sv_early[:, i, :] for i in range(EARLY)] + [late[:] for late in sv_late]
         wd_codes = [sbuf("wd_codes%d" % z, [P, 2 * R], U8) for z in range(2)]
         xs_codes = sbuf("xs_codes", [P, K], U32)
         gs_codes = sbuf("gs_codes", [P, 2 * R], U8)
 
-        def load_rows(raw, rows, cols):
-            nc.sync.dma_start(out=raw[:], in_=rows.rearrange("(p j) w -> p j w", j=PACK)[:, :, cols])
+        def load_half(raw, rows, h):
+            nc.sync.dma_start(out=raw[:], in_=rows.rearrange("(p j) w -> p j w", j=PACK)[:, :, half_cols(h)])
 
         def load_g(z, h):
-            load_rows(g_raw[z][h], g[512 * z : 512 * (z + 1), :], slice(G_CUTS[z][h], G_CUTS[z][h + 1]))
-
-        def load_xr(h):
-            load_rows(xr_raw[h], xr, slice(HALF * h, HALF * (h + 1)))
+            load_half(g_raw[z][h], g[PASS * z : PASS * (z + 1), :], h)
 
         def load_sv(i):
-            nc.sync.dma_start(out=sv_raw[i][:], in_=sv[i * P : (i + 1) * P, :])
+            nc.sync.dma_start(out=sv_raw[i], in_=sv[tile_cols(i), :])
 
-        def load_rw():
-            nc.scalar.dma_start(out=rw_col[:], in_=rw[0].rearrange("(p j) -> p j", j=PACK))
-
-        def load_bytes(codes, words):
+        def load_codes(codes, words):
             nc.sync.dma_start(out=codes[:].bitcast(I32), in_=words.bitcast(I32))
 
-        def load_plane(plane, scales, queue):
+        def load_plane(queue, plane, scales):
             for q in range(4):
                 queue.dma_start(
-                    out=plane[32 * q : 32 * q + 4].bitcast(I32),
-                    in_=scales[4 * q : 4 * q + 4].bitcast(I32),
+                    out=plane[32 * q : 32 * q + 4].bitcast(I32), in_=scales[4 * q : 4 * q + 4].bitcast(I32)
                 )
 
-        load_plane(xs_plane, xs_scales[0], nc.gpsimd)
-        load_plane(gs_plane, gs_scales[0], nc.gpsimd)
-        load_rw()
-        nc.sync.dma_start(out=sv_early[:], in_=sv[0 : 2 * P, :].rearrange("(i p) t -> p i t", p=P))
+        load_plane(nc.gpsimd, xs_plane, xs_scales[0])
+        nc.scalar.dma_start(out=rw_col[:], in_=rw[0].rearrange("(p j) -> p j", j=PACK))
+        nc.sync.dma_start(out=sv_early[:], in_=sv[0 : EARLY * P, :].rearrange("(i p) t -> p i t", p=P))
         load_g(0, 0)
         load_g(0, 1)
-        load_bytes(wd_codes[0], wd_words[0])
-        load_plane(wd_plane, wd_scales.rearrange("z q c -> q z c"), nc.scalar)
+        load_plane(nc.scalar, wd_plane, wd_scales.rearrange("z q c -> q z c"))
         load_g(1, 0)
+        load_codes(wd_codes[0], wd_words[0])
         load_g(1, 1)
-        load_bytes(wd_codes[1], wd_words[1])
-        load_sv(2)
-        load_sv(3)
-        load_xr(0)
-        load_bytes(xs_codes, xs_words[0].rearrange("p c t -> p (c t)"))
-        load_bytes(gs_codes, gs_words[0])
-        load_xr(1)
+        load_sv(GPSIMD_GATE)
+        load_codes(wd_codes[1], wd_words[1])
+        load_sv(VECTOR_GATE)
+        load_half(xr_raw[0], xr, 0)
+        load_plane(nc.sync, gs_plane, gs_scales[0])
+        load_codes(xs_codes, xs_words[0].rearrange("p c j -> p (c j)"))
+        load_codes(gs_codes, gs_words[0])
+        load_half(xr_raw[1], xr, 1)
 
-        rw_all = ps.tile([P, PACK, P], F32, name="rw_all", tag="w3")
-        g_bf = [
-            [sbuf("g_bf%d%d" % (z, h), [P, cuts[h + 1] - cuts[h], PACK], BF16) for h in range(len(cuts) - 1)]
-            for z, cuts in enumerate(G_CUTS)
-        ]
+        rw_bank = ps.tile([P, PACK, P], F32, name="rw_bank", tag="w3")
+        d_bank = [ps.tile([P, T], F32, name="d%d" % i, tag="d%d" % i) for i in range(TILES)]
+        turned = {}
+        w_bank = {}
+        g_bf = [[sbuf("g_bf%d%d" % (z, h), [P, HALF, PACK], BF16) for h in range(2)] for z in range(2)]
         g_codes = [sbuf("g_codes%d" % z, [P, T], U32) for z in range(2)]
         g_plane = [sbuf("g_plane%d" % z, [P, T], U8) for z in range(2)]
-        d_bank = [ps.tile([P, T], F32, name="d%d" % i, tag="d%d" % i) for i in range(TILES)]
+        rw_row = sbuf("rw_row", [P, T], F32)
+        sv_pos = sbuf("sv_pos", [P, T], F32)
         gate = [sbuf("gate%d" % i, [P, T], F32) for i in range(TILES)]
         dz = [sbuf("dz%d" % i, [P, T], BF16) for i in range(TILES)]
         dt_bf = [sbuf("dt_bf%d" % i, [P, P, PACK], BF16) for i in range(TILES)]
         dt_codes = sbuf("dt_codes", [P, R], U32)
         dt_plane = sbuf("dt_plane", [P, R], U8)
+        xr_bf = [sbuf("xr_bf%d" % h, [P, HALF, PACK], BF16) for h in range(2)]
         xr_codes = [sbuf("xr_codes%d" % h, [P, HALF], U32) for h in range(2)]
         xr_plane = [sbuf("xr_plane%d" % h, [P, HALF], U8) for h in range(2)]
-        xr_bf = [sbuf("xr_bf%d" % h, [P, HALF, PACK], BF16) for h in range(2)]
-        turned = {}
-        w_bank = {}
 
-        def spread_rw():
-            for j in range(PACK):
-                nc.tensor.transpose(rw_all[:, j, :], rw_col[:, j : j + 1].to_broadcast([P, P]), ident[:])
+        def pair_order(ap):
+            return ap.rearrange("p (u m e) -> p u m e", u=2, e=2)
+
+        def to_pair_order(ap):
+            return ap.rearrange("p (m u e) -> p u m e", u=2, e=2)
 
         def interleave(copy, grouped, raw, c0, c1):
             copy(
@@ -132,24 +133,15 @@ def tile_mix_first_layer_wgrad_with_store_kernel(
                 in_=raw[:, :, c0:c1].rearrange("p j (c i) -> p c j i", i=4),
             )
 
-        def cast(grouped, raw, share):
-            if share > 0:
-                interleave(nc.vector.tensor_copy, grouped, raw, 0, share)
-            if share < raw.shape[2]:
-                interleave(nc.scalar.copy, grouped, raw, share, raw.shape[2])
+        def cast_shared(grouped, raw):
+            interleave(nc.vector.tensor_copy, grouped, raw, 0, CAST_SHARE)
+            interleave(nc.scalar.copy, grouped, raw, CAST_SHARE, HALF)
 
         def quantize(grouped, codes, plane, fmt):
             nc.vector.quantize_mx(out=codes.bitcast(fmt), scales=plane, in_=grouped[:].rearrange("p c j -> p (c j)"))
 
-        def cast_g(z, h, share):
-            cast(g_bf[z][h], g_raw[z][h], share)
-
         def quantize_g(z, h):
-            cols = slice(G_CUTS[z][h], G_CUTS[z][h + 1])
-            quantize(g_bf[z][h], g_codes[z][:, cols], g_plane[z][:, cols], E5M2)
-
-        def cast_xr(h, share):
-            cast(xr_bf[h], xr_raw[h], share)
+            quantize(g_bf[z][h], g_codes[z][:, half_cols(h)], g_plane[z][:, half_cols(h)], E5M2)
 
         def quantize_xr(h):
             quantize(xr_bf[h], xr_codes[h][:], xr_plane[h][:], E4M3)
@@ -158,71 +150,47 @@ def tile_mix_first_layer_wgrad_with_store_kernel(
             nc.tensor.matmul_mx(
                 out=d_bank[i][:],
                 lhsT=wd_codes[z][:, 2 * P * i : 2 * P * (i + 1)].bitcast(E2M1),
-                lhsT_scale=wd_plane[:, z, P * i : P * (i + 1)],
+                lhsT_scale=wd_plane[:, z, tile_cols(i)],
                 rhs=g_codes[z][:].bitcast(E5M2),
                 rhs_scale=g_plane[z][:],
                 start=(z == 0),
                 stop=(z == 1),
             )
 
-        def make_gate(i):
+        def vector_gate(i):
             for u in range(2):
                 nc.vector.scalar_tensor_tensor(
-                    out=gate[i][:, HALF * u : HALF * (u + 1)].rearrange("p (m e) -> p m e", e=2),
-                    in0=sv_raw[i][:].rearrange("p (m j) -> p m j", j=PACK)[:, :, 2 * u : 2 * u + 2],
+                    out=pair_order(gate[i][:])[:, u],
+                    in0=to_pair_order(sv_raw[i])[:, u],
                     scalar=0.0,
-                    in1=rw_all[:, 2 * u : 2 * u + 2, :].rearrange("p e m -> p m e"),
+                    in1=rw_bank[:, 2 * u : 2 * u + 2, :].rearrange("p e m -> p m e"),
                     op0=ALU.max,
                     op1=ALU.mult,
                 )
 
-        rw_row = sbuf("rw_row", [P, T], F32)
-        sv_pos = sbuf("sv_pos", [P, T], F32)
-
-        def fetch_rw():
-            nc.scalar.copy(
-                out=rw_row[:].rearrange("p (u m e) -> p u m e", u=2, e=2),
-                in_=rw_all[:].rearrange("p (u e) m -> p u m e", e=2),
-            )
-
-        def relu(i):
-            nc.scalar.activation(
-                out=sv_pos[:].rearrange("p (u m e) -> p u m e", u=2, e=2),
-                in_=sv_raw[i][:].rearrange("p (m u e) -> p u m e", u=2, e=2),
-                func=ACT.Relu,
-            )
-
-        def pool_gate(i):
-            nc.gpsimd.tensor_tensor(out=gate[i][:], in0=sv_pos[:], in1=rw_row[:], op=ALU.mult)
-
         def make_dz(i):
             nc.vector.tensor_tensor(
-                out=dz[i][:].rearrange("p (u m e) -> p u m e", u=2, e=2),
-                in0=d_bank[i][:].rearrange("p (m u e) -> p u m e", u=2, e=2),
-                in1=gate[i][:].rearrange("p (u m e) -> p u m e", u=2, e=2),
-                op=ALU.mult,
+                out=pair_order(dz[i][:]), in0=to_pair_order(d_bank[i][:]), in1=pair_order(gate[i][:]), op=ALU.mult
             )
 
         def turn(i):
             words = dz[i][:].bitcast(F32)
             turned[i] = ps.tile([P, 2, P], F32, name="turned%d" % i, tag="d%d" % i)
             for u in range(2):
-                nc.tensor.transpose(turned[i][:, u, :], words[:, P * u : P * (u + 1)], ident[:])
+                nc.tensor.transpose(turned[i][:, u, :], words[:, tile_cols(u)], ident[:])
 
-        def fetch(i):
-            nc.scalar.copy(out=dt_bf[i][:].bitcast(F32), in_=turned[i][:].rearrange("p u r -> p r u"))
+        def fetch(copy, i):
+            copy(out=dt_bf[i][:].bitcast(F32), in_=turned[i][:].rearrange("p u r -> p r u"))
 
         def quantize_dt(i):
-            cols = slice(i * P, (i + 1) * P)
-            quantize(dt_bf[i], dt_codes[:, cols], dt_plane[:, cols], E5M2)
+            quantize(dt_bf[i], dt_codes[:, tile_cols(i)], dt_plane[:, tile_cols(i)], E5M2)
 
         def stored_pass(i):
-            cols = slice(i * P, (i + 1) * P)
             w_bank[i] = ps.tile([P, R], F32, name="w%d" % i, tag="w%d" % i)
             nc.tensor.matmul_mx(
                 out=w_bank[i][:],
-                lhsT=xs_codes[:, cols].bitcast(E4M3),
-                lhsT_scale=xs_plane[:, cols],
+                lhsT=xs_codes[:, tile_cols(i)].bitcast(E4M3),
+                lhsT_scale=xs_plane[:, tile_cols(i)],
                 rhs=gs_codes[:].bitcast(E2M1),
                 rhs_scale=gs_plane[:],
                 start=True,
@@ -230,81 +198,76 @@ def tile_mix_first_layer_wgrad_with_store_kernel(
             )
 
         def fresh_pass(i):
-            cols = slice((i % 2) * P, (i % 2 + 1) * P)
+            h, within = divmod(i, 2)
             nc.tensor.matmul_mx(
                 out=w_bank[i][:],
-                lhsT=xr_codes[i // 2][:, cols].bitcast(E4M3),
-                lhsT_scale=xr_plane[i // 2][:, cols],
+                lhsT=xr_codes[h][:, tile_cols(within)].bitcast(E4M3),
+                lhsT_scale=xr_plane[h][:, tile_cols(within)],
                 rhs=dt_codes[:].bitcast(E5M2),
                 rhs_scale=dt_plane[:],
                 start=False,
                 stop=True,
             )
 
-        def store(i):
-            cuts = OUT_CUTS[i]
-            for c0, c1 in zip(cuts, cuts[1:]):
-                result = sbuf("result%d_%d" % (i, c0), [P, c1 - c0], F32)
-                if i % 2 == 0:
-                    nc.scalar.activation(out=result[:], in_=w_bank[i][:, c0:c1], func=ACT.Copy, scale=OUT_SCALE)
-                else:
-                    nc.vector.tensor_scalar(
-                        out=result[:], in0=w_bank[i][:, c0:c1], scalar1=OUT_SCALE, scalar2=None, op0=ALU.mult
-                    )
-                nc.sync.dma_start(out=out[i * P : (i + 1) * P, c0:c1], in_=result[:])
+        def store(i, cols):
+            result = sbuf("result%d_%d" % (i, cols.start), [P, cols.stop - cols.start], F32)
+            if i % 2 == 0:
+                nc.scalar.activation(out=result[:], in_=w_bank[i][:, cols], func=ACT.Copy, scale=OUT_SCALE)
+            else:
+                nc.vector.tensor_scalar(
+                    out=result[:], in0=w_bank[i][:, cols], scalar1=OUT_SCALE, scalar2=None, op0=ALU.mult
+                )
+            nc.sync.dma_start(out=out[tile_cols(i), cols], in_=result[:])
 
-        spread_rw()
-        make_gate(0)
-        make_gate(1)
-        cast_g(0, 0, 128)
+        for j in range(PACK):
+            nc.tensor.transpose(rw_bank[:, j, :], rw_col[:, j : j + 1].to_broadcast([P, P]), ident[:])
+        for i in range(EARLY):
+            vector_gate(i)
+        interleave(nc.scalar.copy, g_bf[0][0], g_raw[0][0], 0, HALF)
+        cast_shared(g_bf[0][1], g_raw[0][1])
         quantize_g(0, 0)
-        cast_g(0, 1, 160)
         quantize_g(0, 1)
-        fetch_rw()
-        d_pass(0, 0)
-        d_pass(1, 0)
-        d_pass(2, 0)
-        d_pass(3, 0)
-        cast_g(1, 0, 160)
-        quantize_g(1, 0)
-        cast_g(1, 1, 160)
-        quantize_g(1, 1)
-        d_pass(0, 1)
-        d_pass(1, 1)
-        d_pass(2, 1)
-        d_pass(3, 1)
-        relu(3)
-        pool_gate(3)
-        make_gate(2)
-        cast_xr(0, 0)
-        make_dz(0)
-        turn(0)
-        make_dz(1)
-        turn(1)
-        make_dz(2)
-        turn(2)
-        stored_pass(0)
-        make_dz(3)
-        turn(3)
-        stored_pass(1)
-        stored_pass(2)
-        fetch(0)
-        fetch(1)
-        fetch(2)
-        fetch(3)
+        nc.scalar.copy(out=pair_order(rw_row[:]), in_=rw_bank[:].rearrange("p (u e) m -> p u m e", e=2))
+        for h in range(2):
+            cast_shared(g_bf[1][h], g_raw[1][h])
+            quantize_g(1, h)
+
+        last = TILES - 1
+        for i in range(last):
+            d_pass(i, 0)
+        for i in range(last):
+            d_pass(i, 1)
+        d_pass(last, 0)
+        d_pass(last, 1)
+
+        nc.scalar.activation(out=pair_order(sv_pos[:]), in_=to_pair_order(sv_raw[GPSIMD_GATE]), func=ACT.Relu)
+        nc.gpsimd.tensor_tensor(out=gate[GPSIMD_GATE][:], in0=sv_pos[:], in1=rw_row[:], op=ALU.mult)
+        vector_gate(VECTOR_GATE)
+
+        interleave(nc.scalar.copy, xr_bf[0], xr_raw[0], 0, HALF)
+        for i in range(TILES):
+            make_dz(i)
+        for pair in range(2):
+            for i in (2 * pair, 2 * pair + 1):
+                turn(i)
+            for i in (2 * pair, 2 * pair + 1):
+                stored_pass(i)
+
+        fetch(nc.scalar.copy, 0)
+        fetch(nc.scalar.copy, 1)
+        fetch(nc.scalar.copy, 3)
         quantize_xr(0)
         quantize_dt(0)
         quantize_dt(1)
+        fetch(nc.vector.tensor_copy, 2)
         quantize_dt(2)
         quantize_dt(3)
-        cast_xr(1, 160)
+        cast_shared(xr_bf[1], xr_raw[1])
         quantize_xr(1)
+
         fresh_pass(0)
-        store(0)
-        fresh_pass(1)
-        store(1)
-        fresh_pass(2)
-        store(2)
-        stored_pass(3)
-        fresh_pass(3)
-        store(3)
+        store(0, half_cols(0))
+        store(0, half_cols(1))
+        for i in range(1, TILES):
+            fresh_pass(i)
+            store(i, slice(0, R))

from contextlib import ExitStack

import concourse.mybir as mybir
from concourse.masks import make_identity

K, R, N, T, S = 512, 512, 1024, 512, 512
FLOPS = 2 * (N * R * T + T * K * R + S * K * R)

F32 = mybir.dt.float32
BF16 = mybir.dt.bfloat16
I32 = mybir.dt.int32
U32 = mybir.dt.uint32
U8 = mybir.dt.uint8
E4M3 = mybir.dt.float8_e4m3fn_x4
E5M2 = mybir.dt.float8_e5m2_x4
E2M1 = mybir.dt.float4_e2m1fn_x4
ALU = mybir.AluOpType
ACT = mybir.ActivationFunctionType

P = 128
PACK = 4
PASS = P * PACK
HALF = 256
TILES = 4
EARLY = 2
VECTOR_GATE = 2
GPSIMD_GATE = 3
CAST_SHARE = 160
OUT_SCALE = 0.04


def tile_mix_first_layer_wgrad_with_store_kernel(
    tc, xr, g, wd_words, wd_scales, sv, rw, xs_words, xs_scales, gs_words, gs_scales, out
):
    nc = tc.nc
    with ExitStack() as ctx:
        sb = ctx.enter_context(tc.tile_pool(name="sb", bufs=1))
        ps = ctx.enter_context(tc.psum_pool(name="ps", bufs=1))
        ctx.enter_context(tc.manual_schedule())

        def sbuf(name, shape, dtype):
            return sb.tile(shape, dtype, name=name, align_bytes=64)

        def tile_cols(i):
            return slice(P * i, P * (i + 1))

        def half_cols(h):
            return slice(HALF * h, HALF * (h + 1))

        ident = sbuf("ident", [P, P], F32)
        make_identity(nc, ident[:])

        wd_plane = sbuf("wd_plane", [P, 2, R], U8)
        xs_plane = sbuf("xs_plane", [P, K], U8)
        gs_plane = sbuf("gs_plane", [P, R], U8)
        nc.vector.memset(wd_plane[:].rearrange("p z c -> p (z c)").bitcast(I32), 0)
        nc.vector.memset(xs_plane[:].bitcast(I32), 0)
        nc.vector.memset(gs_plane[:].bitcast(I32), 0)

        rw_col = sbuf("rw_col", [P, PACK], F32)
        g_raw = [[sbuf("g_raw%d%d" % (z, h), [P, PACK, HALF], F32) for h in range(2)] for z in range(2)]
        xr_raw = [sbuf("xr_raw%d" % h, [P, PACK, HALF], F32) for h in range(2)]
        sv_early = sbuf("sv_early", [P, EARLY, T], F32)
        sv_late = [sbuf("sv_late%d" % i, [P, T], F32) for i in range(EARLY, TILES)]
        sv_raw = [sv_early[:, i, :] for i in range(EARLY)] + [late[:] for late in sv_late]
        wd_codes = [sbuf("wd_codes%d" % z, [P, 2 * R], U8) for z in range(2)]
        xs_codes = sbuf("xs_codes", [P, K], U32)
        gs_codes = sbuf("gs_codes", [P, 2 * R], U8)

        def load_half(raw, rows, h):
            nc.sync.dma_start(out=raw[:], in_=rows.rearrange("(p j) w -> p j w", j=PACK)[:, :, half_cols(h)])

        def load_g(z, h):
            load_half(g_raw[z][h], g[PASS * z : PASS * (z + 1), :], h)

        def load_sv(i):
            nc.sync.dma_start(out=sv_raw[i], in_=sv[tile_cols(i), :])

        def load_codes(codes, words):
            nc.sync.dma_start(out=codes[:].bitcast(I32), in_=words.bitcast(I32))

        def load_plane(queue, plane, scales):
            for q in range(4):
                queue.dma_start(
                    out=plane[32 * q : 32 * q + 4].bitcast(I32), in_=scales[4 * q : 4 * q + 4].bitcast(I32)
                )

        load_plane(nc.gpsimd, xs_plane, xs_scales[0])
        nc.scalar.dma_start(out=rw_col[:], in_=rw[0].rearrange("(p j) -> p j", j=PACK))
        nc.sync.dma_start(out=sv_early[:], in_=sv[0 : EARLY * P, :].rearrange("(i p) t -> p i t", p=P))
        load_g(0, 0)
        load_g(0, 1)
        load_plane(nc.scalar, wd_plane, wd_scales.rearrange("z q c -> q z c"))
        load_g(1, 0)
        load_codes(wd_codes[0], wd_words[0])
        load_g(1, 1)
        load_sv(GPSIMD_GATE)
        load_codes(wd_codes[1], wd_words[1])
        load_sv(VECTOR_GATE)
        load_half(xr_raw[0], xr, 0)
        load_plane(nc.sync, gs_plane, gs_scales[0])
        load_codes(xs_codes, xs_words[0].rearrange("p c j -> p (c j)"))
        load_codes(gs_codes, gs_words[0])
        load_half(xr_raw[1], xr, 1)

        rw_bank = ps.tile([P, PACK, P], F32, name="rw_bank", tag="w3")
        d_bank = [ps.tile([P, T], F32, name="d%d" % i, tag="d%d" % i) for i in range(TILES)]
        turned = {}
        w_bank = {}
        g_bf = [[sbuf("g_bf%d%d" % (z, h), [P, HALF, PACK], BF16) for h in range(2)] for z in range(2)]
        g_codes = [sbuf("g_codes%d" % z, [P, T], U32) for z in range(2)]
        g_plane = [sbuf("g_plane%d" % z, [P, T], U8) for z in range(2)]
        rw_row = sbuf("rw_row", [P, T], F32)
        sv_pos = sbuf("sv_pos", [P, T], F32)
        gate = [sbuf("gate%d" % i, [P, T], F32) for i in range(TILES)]
        dz = [sbuf("dz%d" % i, [P, T], BF16) for i in range(TILES)]
        dt_bf = [sbuf("dt_bf%d" % i, [P, P, PACK], BF16) for i in range(TILES)]
        dt_codes = sbuf("dt_codes", [P, R], U32)
        dt_plane = sbuf("dt_plane", [P, R], U8)
        xr_bf = [sbuf("xr_bf%d" % h, [P, HALF, PACK], BF16) for h in range(2)]
        xr_codes = [sbuf("xr_codes%d" % h, [P, HALF], U32) for h in range(2)]
        xr_plane = [sbuf("xr_plane%d" % h, [P, HALF], U8) for h in range(2)]

        def pair_order(ap):
            return ap.rearrange("p (u m e) -> p u m e", u=2, e=2)

        def to_pair_order(ap):
            return ap.rearrange("p (m u e) -> p u m e", u=2, e=2)

        def interleave(copy, grouped, raw, c0, c1):
            copy(
                out=grouped[:, c0:c1, :].rearrange("p (c i) j -> p c j i", i=4),
                in_=raw[:, :, c0:c1].rearrange("p j (c i) -> p c j i", i=4),
            )

        def cast_shared(grouped, raw):
            interleave(nc.vector.tensor_copy, grouped, raw, 0, CAST_SHARE)
            interleave(nc.scalar.copy, grouped, raw, CAST_SHARE, HALF)

        def quantize(grouped, codes, plane, fmt):
            nc.vector.quantize_mx(out=codes.bitcast(fmt), scales=plane, in_=grouped[:].rearrange("p c j -> p (c j)"))

        def quantize_g(z, h):
            quantize(g_bf[z][h], g_codes[z][:, half_cols(h)], g_plane[z][:, half_cols(h)], E5M2)

        def quantize_xr(h):
            quantize(xr_bf[h], xr_codes[h][:], xr_plane[h][:], E4M3)

        def d_pass(i, z):
            nc.tensor.matmul_mx(
                out=d_bank[i][:],
                lhsT=wd_codes[z][:, 2 * P * i : 2 * P * (i + 1)].bitcast(E2M1),
                lhsT_scale=wd_plane[:, z, tile_cols(i)],
                rhs=g_codes[z][:].bitcast(E5M2),
                rhs_scale=g_plane[z][:],
                start=(z == 0),
                stop=(z == 1),
            )

        def vector_gate(i):
            for u in range(2):
                nc.vector.scalar_tensor_tensor(
                    out=pair_order(gate[i][:])[:, u],
                    in0=to_pair_order(sv_raw[i])[:, u],
                    scalar=0.0,
                    in1=rw_bank[:, 2 * u : 2 * u + 2, :].rearrange("p e m -> p m e"),
                    op0=ALU.max,
                    op1=ALU.mult,
                )

        def make_dz(i):
            nc.vector.tensor_tensor(
                out=pair_order(dz[i][:]), in0=to_pair_order(d_bank[i][:]), in1=pair_order(gate[i][:]), op=ALU.mult
            )

        def turn(i):
            words = dz[i][:].bitcast(F32)
            turned[i] = ps.tile([P, 2, P], F32, name="turned%d" % i, tag="d%d" % i)
            for u in range(2):
                nc.tensor.transpose(turned[i][:, u, :], words[:, tile_cols(u)], ident[:])

        def fetch(copy, i):
            copy(out=dt_bf[i][:].bitcast(F32), in_=turned[i][:].rearrange("p u r -> p r u"))

        def quantize_dt(i):
            quantize(dt_bf[i], dt_codes[:, tile_cols(i)], dt_plane[:, tile_cols(i)], E5M2)

        def stored_pass(i):
            w_bank[i] = ps.tile([P, R], F32, name="w%d" % i, tag="w%d" % i)
            nc.tensor.matmul_mx(
                out=w_bank[i][:],
                lhsT=xs_codes[:, tile_cols(i)].bitcast(E4M3),
                lhsT_scale=xs_plane[:, tile_cols(i)],
                rhs=gs_codes[:].bitcast(E2M1),
                rhs_scale=gs_plane[:],
                start=True,
                stop=False,
            )

        def fresh_pass(i):
            h, within = divmod(i, 2)
            nc.tensor.matmul_mx(
                out=w_bank[i][:],
                lhsT=xr_codes[h][:, tile_cols(within)].bitcast(E4M3),
                lhsT_scale=xr_plane[h][:, tile_cols(within)],
                rhs=dt_codes[:].bitcast(E5M2),
                rhs_scale=dt_plane[:],
                start=False,
                stop=True,
            )

        def store(i, cols):
            result = sbuf("result%d_%d" % (i, cols.start), [P, cols.stop - cols.start], F32)
            if i % 2 == 0:
                nc.scalar.activation(out=result[:], in_=w_bank[i][:, cols], func=ACT.Copy, scale=OUT_SCALE)
            else:
                nc.vector.tensor_scalar(
                    out=result[:], in0=w_bank[i][:, cols], scalar1=OUT_SCALE, scalar2=None, op0=ALU.mult
                )
            nc.sync.dma_start(out=out[tile_cols(i), cols], in_=result[:])

        for j in range(PACK):
            nc.tensor.transpose(rw_bank[:, j, :], rw_col[:, j : j + 1].to_broadcast([P, P]), ident[:])
        for i in range(EARLY):
            vector_gate(i)
        interleave(nc.scalar.copy, g_bf[0][0], g_raw[0][0], 0, HALF)
        cast_shared(g_bf[0][1], g_raw[0][1])
        quantize_g(0, 0)
        quantize_g(0, 1)
        nc.scalar.copy(out=pair_order(rw_row[:]), in_=rw_bank[:].rearrange("p (u e) m -> p u m e", e=2))
        for h in range(2):
            cast_shared(g_bf[1][h], g_raw[1][h])
            quantize_g(1, h)

        last = TILES - 1
        for i in range(last):
            d_pass(i, 0)
        for i in range(last):
            d_pass(i, 1)
        d_pass(last, 0)
        d_pass(last, 1)

        nc.scalar.activation(out=pair_order(sv_pos[:]), in_=to_pair_order(sv_raw[GPSIMD_GATE]), func=ACT.Relu)
        nc.gpsimd.tensor_tensor(out=gate[GPSIMD_GATE][:], in0=sv_pos[:], in1=rw_row[:], op=ALU.mult)
        vector_gate(VECTOR_GATE)

        interleave(nc.scalar.copy, xr_bf[0], xr_raw[0], 0, HALF)
        for i in range(TILES):
            make_dz(i)
        for pair in range(2):
            for i in (2 * pair, 2 * pair + 1):
                turn(i)
            for i in (2 * pair, 2 * pair + 1):
                stored_pass(i)

        fetch(nc.scalar.copy, 0)
        fetch(nc.scalar.copy, 1)
        fetch(nc.scalar.copy, 3)
        quantize_xr(0)
        quantize_dt(0)
        quantize_dt(1)
        fetch(nc.vector.tensor_copy, 2)
        quantize_dt(2)
        quantize_dt(3)
        cast_shared(xr_bf[1], xr_raw[1])
        quantize_xr(1)

        fresh_pass(0)
        store(0, half_cols(0))
        store(0, half_cols(1))
        for i in range(1, TILES):
            fresh_pass(i)
            store(i, slice(0, R))
